import numpy as np
import ml_dtypes


def mxq(x, axis, fmt="e4m3"):
    dtype, down = {"e4m3": (ml_dtypes.float8_e4m3fn, 7), "e5m2": (ml_dtypes.float8_e5m2, 14)}[fmt]
    v = np.moveaxis(np.asarray(x, np.float32).astype(ml_dtypes.bfloat16).astype(np.float64), axis, -1)
    blocks = v.reshape(v.shape[:-1] + (-1, 32))
    amax = np.abs(blocks).max(-1, keepdims=True)
    byte = np.maximum(np.where(amax > 0, np.frexp(amax)[1] - 1 + 127, 0) - down, 1)
    scale = np.exp2(byte - 127.0)
    codes = (blocks / scale).astype(np.float32).astype(dtype).astype(np.float64)
    return np.moveaxis((codes * scale).reshape(v.shape), -1, axis)


WIDE = False


def mx_kscale(k):
    if not WIDE:
        return np.ones(k)
    levels = np.array([10, -10, 5, -5, 0])
    if k % 512:
        return np.exp2(np.random.permutation(np.resize(levels, k // 32))).repeat(32)
    a = np.empty((k // 512, 16))
    for p in range(k // 512):
        a[p, :8] = np.random.permutation(np.resize(levels, 8))
        for g in range(8):
            far = levels[np.abs(levels - a[p, g]) >= 10]
            a[p, g + 8] = far[np.random.randint(len(far))]
    return np.exp2(a.ravel()).repeat(32)


def f64(x):
    return np.asarray(x).astype(np.float64)


def striped(idx):
    return np.tile(np.asarray(idx).reshape(-1, 16).T, (8, 1)).astype(np.uint16)


def unstriped(offs):
    return offs[:16].T.reshape(-1).astype(np.int64)


def striped8(idx):
    return np.asarray(idx).reshape(8, -1, 16).transpose(0, 2, 1).reshape(128, -1).astype(np.uint16)


def unstriped8(offs):
    return offs.reshape(8, 16, -1).transpose(0, 2, 1).reshape(8, -1).astype(np.int64)


def pick8(x, idx, run):
    r = np.arange(len(x))
    return x[r[:, None], idx[r % (8 * run) // run]]


E2M1 = np.array([0.0, 0.5, 1.0, 1.5, 2.0, 3.0, 4.0, 6.0, -0.0, -0.5, -1.0, -1.5, -2.0, -3.0, -4.0, -6.0])


def pack_weight(w, fmt):
    k, n = w.shape
    w = f64(np.asarray(w, np.float32).astype(ml_dtypes.bfloat16)).reshape(k // 32, 32, n)
    amax = np.abs(w).max(1)
    if fmt == "e4m3":
        byte = np.frexp(amax)[1] - 1 + 127 - 7
    else:
        mant, ex = np.frexp(amax / 6.0)
        byte = np.where(mant > 0.5, ex, ex - 1) + 127
    byte = np.clip(np.where(amax > 0, byte, 1), 1, 254)
    scaled = (w * np.exp2(127.0 - byte)[:, None, :]).reshape(k, n).astype(np.float32)
    by_word = np.ascontiguousarray(scaled.reshape(k // 512, 128, 4, n).transpose(0, 1, 3, 2))
    if fmt == "e4m3":
        words = by_word.astype(ml_dtypes.float8_e4m3fn).view(np.uint8)
    else:
        c = by_word.astype(ml_dtypes.float4_e2m1fn).view(np.uint8) & 0xF
        words = (c[..., 0::2] | (c[..., 1::2] << 4)).reshape(k // 512, 128, 2 * n)
    return np.ascontiguousarray(words), np.ascontiguousarray(byte.astype(np.uint8).reshape(k // 512, 16, n))


def unpack_weight(words, scales, fmt):
    g, _, n = scales.shape
    words = np.ascontiguousarray(words).reshape(g, 128, n, -1)
    if fmt == "e4m3":
        vals = words.view(ml_dtypes.float8_e4m3fn).astype(np.float64)
    else:
        nib = np.empty((g, 128, n, 4), np.uint8)
        nib[..., 0::2] = words & 0xF
        nib[..., 1::2] = words >> 4
        vals = E2M1[nib]
    vals = vals * np.repeat(np.exp2(scales.astype(np.float64) - 127.0), 8, axis=1)[..., None]
    return vals.transpose(0, 1, 3, 2).reshape(g * 512, n)


K, J, R, T, U, F, C, O, N, S, Z = 512, 256, 512, 1024, 512, 1024, 512, 128, 256, 512, 1024


def setup_inputs():
    n = np.random.standard_normal
    idx = np.stack([np.random.permutation(T)[:U] for _ in range(8)])
    idx2 = np.random.permutation(U)[:J]
    idx3 = np.stack([np.random.permutation(F)[:R] for _ in range(8)])
    idx4 = np.random.permutation(C)[:J]
    idx5 = np.random.permutation(C)[:O]
    idx6 = np.stack([np.random.permutation(C)[:O] for _ in range(8)])
    idx7 = np.random.permutation(Z)[:O]
    fk = mx_kscale(K)
    fr = mx_kscale(R)
    fs = mx_kscale(S)
    wbp = pack_weight(n((R, N)) * 1 / np.sqrt(R) / fr[:, None], "e4m3")
    xrp = pack_weight(n((S, Z)) / fs[:, None], "e4m3")
    wsp = pack_weight(n((S, N)) * 1 / np.sqrt(S) * fs[:, None], "e2m1")
    return {
        "ta": (np.random.randint(-7, 8, (K, T)).astype(np.float64)).astype(np.float32),
        "ga": ((np.random.randint(8, 25, (K, 1)) / 64.0) * fk[:, None]).astype(np.float32),
        "gb": (np.random.uniform(0.5, 1.6, (K, 1))).astype(np.float32),
        "ua": (np.random.randint(-7, 8, (K, F)).astype(np.float64)).astype(np.float32),
        "ha": ((np.random.randint(8, 25, (K, 1)) / 1024.0) / fk[:, None]).astype(np.float32),
        "sa": (np.random.uniform(0.5, 1.6, (R, 1)) * fr[:, None]).astype(np.float32),
        "sb": (np.random.uniform(0.5, 1.6, (R, 1)) * fr[:, None]).astype(np.float32),
        "wb_words": wbp[0],
        "wb_scales": wbp[1],
        "xr_words": xrp[0],
        "xr_scales": xrp[1],
        "ws_words": wsp[0],
        "ws_scales": wsp[1],
        "offs": striped8(idx),
        "offs2": striped(idx2),
        "offs3": striped8(idx3),
        "offs4": striped(idx4),
        "offs5": striped(idx5),
        "offs6": striped8(idx6),
        "offs7": striped(idx7),
    }


def reference(ta, ga, gb, ua, ha, sa, sb, wb_words, wb_scales, xr_words, xr_scales, ws_words, ws_scales, offs, offs2, offs3, offs4, offs5, offs6, offs7):
    idx = unstriped8(offs)
    idx2 = unstriped(offs2)
    idx3 = unstriped8(offs3)
    idx4 = unstriped(offs4)
    idx5 = unstriped(offs5)
    idx6 = unstriped8(offs6)
    idx7 = unstriped(offs7)
    wbu = unpack_weight(wb_words, wb_scales, "e4m3")
    xru = unpack_weight(xr_words, xr_scales, "e4m3")
    wsu = unpack_weight(ws_words, ws_scales, "e2m1")
    xcd = pick8(f64(ta), idx, 64) * f64(ga)
    xc = xcd[:, idx2] * f64(gb)
    wc = pick8(f64(ua), idx3, 64) * f64(ha)
    wcq = mxq(wc, 0, "e4m3")
    xcq = mxq(xc, 0, "e4m3")
    a = wcq.T @ xcq
    pw = np.zeros((R, C))
    pw[:, idx4] = a
    hid = np.abs(pw[:, idx5] * f64(sa) - pick8(pw, idx6, 64) * f64(sb))
    hidq = mxq(hid, 0, "e4m3")
    xridx7g = xru[:, idx7]
    y = wbu.T @ hidq + wsu.T @ xridx7g
    return y

@@ -1,0 +1,213 @@
+from contextlib import ExitStack
+
+import concourse.mybir as mybir
+
+K, J, R, T, U, F, C, O, N, S, Z = 512, 256, 512, 1024, 512, 1024, 512, 128, 256, 512, 1024
+FLOPS = 2 * K * R * J + 2 * R * N * O + 2 * S * N * O
+
+F32 = mybir.dt.float32
+BF16 = mybir.dt.bfloat16
+I32 = mybir.dt.int32
+U32 = mybir.dt.uint32
+U16 = mybir.dt.uint16
+U8 = mybir.dt.uint8
+FP8X4 = mybir.dt.float8_e4m3fn_x4
+FP4X4 = mybir.dt.float4_e2m1fn_x4
+ACT = mybir.ActivationFunctionType
+ALU = mybir.AluOpType
+
+P = 128
+PACK = 4
+HALF = J // 2
+
+
+def tile_picked_respelled_codes_one_boardmixed_reminder_plain_kernel(
+    tc, ta, ga, gb, ua, ha, sa, sb, wb_words, wb_scales, xr_words, xr_scales, ws_words, ws_scales,
+    offs, offs2, offs3, offs4, offs5, offs6, offs7, out,
+):
+    nc = tc.nc
+    with ExitStack() as ctx:
+        keep = ctx.enter_context(tc.tile_pool(name="keep", bufs=1))
+        psum = ctx.enter_context(tc.psum_pool(name="psum", bufs=1))
+
+        def load_list(src, name):
+            tile = keep.tile(list(src.shape), U16, name=name)
+            nc.sync.dma_start(tile[:], src)
+            return tile
+
+        def load_factor(queue, src, name):
+            tile = keep.tile([P, PACK], F32, name=name)
+            queue.dma_start(tile[:], src.rearrange("(p t) o -> p (t o)", t=PACK))
+            return tile
+
+        def load_plane(src, t, name):
+            tile = keep.tile([P, src.shape[1]], F32, name=name, align_bytes=64)
+            nc.sync.dma_start(tile[:], src.rearrange("(p t) c -> t p c", t=PACK)[t])
+            return tile
+
+        def load_scales(src, tile):
+            for q in range(4):
+                nc.sync.dma_start(tile[32 * q : 32 * q + 4, :].bitcast(I32), src[0, 4 * q : 4 * q + 4, :].bitcast(I32))
+
+        xr_s = keep.tile([P, Z], U8, align_bytes=64)
+        ws_s = keep.tile([P, N], U8, align_bytes=64)
+        wb_s = keep.tile([P, N], U8, align_bytes=64)
+        for tile in (xr_s, ws_s, wb_s):
+            nc.vector.memset(tile[:].bitcast(I32), 0)
+        board = [keep.tile([P, C], F32, name="board%d" % t) for t in range(PACK)]
+        for t in range(PACK):
+            nc.vector.memset(board[t][:], 0.0)
+
+        ga_t = load_factor(nc.scalar, ga, "ga_t")
+        l1 = load_list(offs, "l1")
+        ta_p, ua_p = {}, {}
+        ta_p[0] = load_plane(ta, 0, "ta0")
+        gb_t = load_factor(nc.scalar, gb, "gb_t")
+        l2 = load_list(offs2, "l2")
+        ha_t = load_factor(nc.scalar, ha, "ha_t")
+        l3 = load_list(offs3, "l3")
+        ua_p[0] = load_plane(ua, 0, "ua0")
+        ta_p[1] = load_plane(ta, 1, "ta1")
+        for t in (1, 2, 3):
+            ua_p[t] = load_plane(ua, t, "ua%d" % t)
+        for t in (2, 3):
+            ta_p[t] = load_plane(ta, t, "ta%d" % t)
+        l4 = load_list(offs4, "l4")
+        xr_w = keep.tile([P, Z], U32, align_bytes=64)
+        nc.sync.dma_start(xr_w[:].bitcast(I32), xr_words[0].rearrange("p n t -> p (n t)").bitcast(I32))
+        l7 = load_list(offs7, "l7")
+        l5 = load_list(offs5, "l5")
+        l6 = load_list(offs6, "l6")
+        sa_t = load_factor(nc.sync, sa, "sa_t")
+        sb_t = load_factor(nc.sync, sb, "sb_t")
+        load_scales(xr_scales, xr_s)
+        ws_w = keep.tile([P, 2 * N], U8, align_bytes=64)
+        nc.sync.dma_start(ws_w[:].bitcast(I32), ws_words[0].bitcast(I32))
+        load_scales(ws_scales, ws_s)
+        wb_w = keep.tile([P, N], U32, align_bytes=64)
+        nc.sync.dma_start(wb_w[:].bitcast(I32), wb_words[0].rearrange("p n t -> p (n t)").bitcast(I32))
+        load_scales(wb_scales, wb_s)
+
+        xcd = [keep.tile([P, U], F32, name="xcd%d" % t) for t in range(PACK)]
+        wc = keep.tile([P, PACK, R], BF16, align_bytes=64)
+        xc = [keep.tile([P, PACK, HALF], BF16, name="xc0", align_bytes=64)]
+
+        def gather_xcd(t):
+            nc.scalar.activation(xcd[t][:], ta_p[t][:].indirect(l1[:]), ACT.Copy, scale=ga_t[:, t : t + 1])
+
+        def gather_xc(h, t):
+            cols = slice(h * HALF // 16, (h + 1) * HALF // 16)
+            nc.scalar.activation(xc[h][:, t, :], xcd[t][:].indirect(l2[:, cols]), ACT.Copy, scale=gb_t[:, t : t + 1])
+
+        def gather_wc(t):
+            nc.scalar.activation(wc[:, t, :], ua_p[t][:].indirect(l3[:]), ACT.Copy, scale=ha_t[:, t : t + 1])
+
+        gather_xcd(0)
+        gather_xc(0, 0)
+        gather_wc(0)
+        gather_xcd(1)
+        gather_xc(0, 1)
+        for t in (1, 2, 3):
+            gather_wc(t)
+        for t in (2, 3):
+            gather_xcd(t)
+            gather_xc(0, t)
+        xc.append(keep.tile([P, PACK, HALF], BF16, name="xc1", tag="ta3", align_bytes=64))
+        for t in range(PACK):
+            gather_xc(1, t)
+
+        wc_i = keep.tile([P, R * PACK], BF16, align_bytes=64)
+        nc.vector.tensor_copy(
+            wc_i[:].rearrange("p (t m i j) -> p m t i j", t=PACK, i=2, j=PACK),
+            wc[:].rearrange("p j (m i t) -> p m t i j", i=2, t=PACK),
+        )
+        wc_w = keep.tile([P, R], U32, align_bytes=64)
+        wc_s = keep.tile([P, R], U8, align_bytes=64)
+        nc.vector.quantize_mx(wc_w[:].bitcast(FP8X4), wc_s[:], wc_i[:])
+
+        a_sb = {}
+
+        def first_product(h):
+            xc_i = keep.tile([P, HALF, PACK], BF16, name="xc_i%d" % h, align_bytes=64)
+            nc.vector.tensor_copy(xc_i[:], xc[h][:].rearrange("p j c -> p c j"))
+            xc_w = keep.tile([P, HALF], U32, name="xc_w%d" % h, align_bytes=64)
+            xc_s = keep.tile([P, HALF], U8, name="xc_s%d" % h, align_bytes=64)
+            nc.vector.quantize_mx(xc_w[:].bitcast(FP8X4), xc_s[:], xc_i[:].rearrange("p c j -> p (c j)"))
+            for pair in range(2):
+                bank = psum.tile([P, 2, HALF], F32, name="a_ps%d%d" % (h, pair))
+                for e in range(2):
+                    cols = slice((2 * pair + e) * P, (2 * pair + e + 1) * P)
+                    nc.tensor.matmul_mx(
+                        bank[:, e, :], lhsT=wc_w[:, cols].bitcast(FP8X4), lhsT_scale=wc_s[:, cols],
+                        rhs=xc_w[:].bitcast(FP8X4), rhs_scale=xc_s[:], start=True, stop=True,
+                    )
+                a_sb[h, pair] = keep.tile([P, 2, HALF], F32, name="a_sb%d%d" % (h, pair))
+                if pair == 0:
+                    nc.vector.tensor_copy(a_sb[h, pair][:], bank[:])
+                else:
+                    nc.scalar.copy(a_sb[h, pair][:], bank[:])
+
+        def scatter(h, t, on_scalar):
+            cols = slice(h * HALF // 16, (h + 1) * HALF // 16)
+            src = a_sb[h, t // 2][:, t % 2, :]
+            if on_scalar:
+                nc.scalar.activation(board[t][:].indirect(l4[:, cols]), src, ACT.Copy)
+            else:
+                nc.vector.tensor_copy(board[t][:].indirect(l4[:, cols]), src)
+
+        diff = keep.tile([P, PACK, O], F32)
+
+        def read_board(t):
+            one = keep.tile([P, O], F32, name="one%d" % t)
+            eight = keep.tile([P, O], F32, name="eight%d" % t)
+            nc.scalar.activation(one[:], board[t][:].indirect(l5[:]), ACT.Copy, scale=sa_t[:, t : t + 1])
+            nc.scalar.activation(eight[:], board[t][:].indirect(l6[:]), ACT.Copy, scale=sb_t[:, t : t + 1])
+            nc.vector.tensor_tensor(diff[:, t, :], one[:], eight[:], ALU.subtract)
+
+        first_product(0)
+        first_product(1)
+        scatter(0, 3, True)
+        scatter(0, 0, False)
+        scatter(0, 2, True)
+        scatter(1, 0, False)
+        scatter(1, 3, True)
+        scatter(0, 1, False)
+        scatter(1, 1, False)
+        scatter(1, 2, False)
+
+        xg_w = keep.tile([P, O], U32, align_bytes=64)
+        xg_s = keep.tile([P, O], U8, align_bytes=64)
+        nc.vector.tensor_copy(xg_w[:], xr_w[:].indirect(l7[:]))
+        nc.vector.tensor_copy(xg_s[:], xr_s[:].indirect(l7[:]))
+        y_ps = [psum.tile([P, O], F32, name="y_ps%d" % h) for h in range(2)]
+        for h in range(2):
+            nc.tensor.matmul_mx(
+                y_ps[h][:], lhsT=ws_w[:, 2 * h * P : 2 * (h + 1) * P].bitcast(FP4X4), lhsT_scale=ws_s[:, h * P : (h + 1) * P],
+                rhs=xg_w[:].bitcast(FP8X4), rhs_scale=xg_s[:], start=True, stop=False,
+            )
+
+        for t in (0, 3, 1, 2):
+            read_board(t)
+
+        hid = keep.tile([P, O, PACK], BF16, align_bytes=64)
+        by_place = diff[:].rearrange("p t o -> p o t")
+        nc.scalar.activation(hid[:, : O // 2, :], by_place[:, : O // 2, :], ACT.Abs)
+        nc.vector.scalar_tensor_tensor(
+            hid[:, O // 2 :, :], by_place[:, O // 2 :, :], -1.0, by_place[:, O // 2 :, :], ALU.mult, ALU.max
+        )
+        hid_w = keep.tile([P, O], U32, align_bytes=64)
+        hid_s = keep.tile([P, O], U8, align_bytes=64)
+        nc.vector.quantize_mx(hid_w[:].bitcast(FP8X4), hid_s[:], hid[:].rearrange("p o t -> p (o t)"))
+        for h in range(2):
+            cols = slice(h * P, (h + 1) * P)
+            nc.tensor.matmul_mx(
+                y_ps[h][:], lhsT=wb_w[:, cols].bitcast(FP8X4), lhsT_scale=wb_s[:, cols],
+                rhs=hid_w[:].bitcast(FP8X4), rhs_scale=hid_s[:], start=False, stop=True,
+            )
+            y_sb = keep.tile([P, O], F32, name="y_sb%d" % h)
+            if h == 0:
+                nc.vector.tensor_copy(y_sb[:], y_ps[h][:])
+                nc.sync.dma_start(out[cols, :], y_sb[:])
+            else:
+                nc.scalar.copy(y_sb[:], y_ps[h][:])
+                nc.scalar.dma_start(out[cols, :], y_sb[:])

@@ -45,9 +45,12 @@ def tile_picked_respelled_codes_one_boardmixed_reminder_plain_kernel(
             nc.sync.dma_start(tile[:], src.rearrange("(p t) c -> t p c", t=PACK)[t])
             return tile
 
-        def load_scales(src, tile):
+        def load_scales(src, tile, name):
+            words = src.shape[2] // 4
+            stage = keep.tile([4, 4, words], I32, name=name)
+            nc.gpsimd.dma_start(stage[:], src[0].bitcast(I32).rearrange("(q r) n -> r q n", r=4))
             for q in range(4):
-                nc.sync.dma_start(tile[32 * q : 32 * q + 4, :].bitcast(I32), src[0, 4 * q : 4 * q + 4, :].bitcast(I32))
+                nc.vector.tensor_copy(tile[32 * q : 32 * q + 4, :].bitcast(I32), stage[:, q, :])
 
         xr_s = keep.tile([P, Z], U8, align_bytes=64)
         ws_s = keep.tile([P, N], U8, align_bytes=64)
@@ -62,31 +65,31 @@ def tile_picked_respelled_codes_one_boardmixed_reminder_plain_kernel(
         l1 = load_list(offs, "l1")
         ta_p, ua_p = {}, {}
         ta_p[0] = load_plane(ta, 0, "ta0")
-        gb_t = load_factor(nc.scalar, gb, "gb_t")
-        l2 = load_list(offs2, "l2")
         ha_t = load_factor(nc.scalar, ha, "ha_t")
+        gb_t = load_factor(nc.scalar, gb, "gb_t")
         l3 = load_list(offs3, "l3")
         ua_p[0] = load_plane(ua, 0, "ua0")
         ta_p[1] = load_plane(ta, 1, "ta1")
+        l7 = load_list(offs7, "l7")
         for t in (1, 2, 3):
             ua_p[t] = load_plane(ua, t, "ua%d" % t)
-        for t in (2, 3):
-            ta_p[t] = load_plane(ta, t, "ta%d" % t)
-        l4 = load_list(offs4, "l4")
-        xr_w = keep.tile([P, Z], U32, align_bytes=64)
-        nc.sync.dma_start(xr_w[:].bitcast(I32), xr_words[0].rearrange("p n t -> p (n t)").bitcast(I32))
-        l7 = load_list(offs7, "l7")
-        l5 = load_list(offs5, "l5")
-        l6 = load_list(offs6, "l6")
-        sa_t = load_factor(nc.sync, sa, "sa_t")
-        sb_t = load_factor(nc.sync, sb, "sb_t")
-        load_scales(xr_scales, xr_s)
         ws_w = keep.tile([P, 2 * N], U8, align_bytes=64)
         nc.sync.dma_start(ws_w[:].bitcast(I32), ws_words[0].bitcast(I32))
-        load_scales(ws_scales, ws_s)
+        for t in (2, 3):
+            ta_p[t] = load_plane(ta, t, "ta%d" % t)
+        l2 = load_list(offs2, "l2")
+        xr_w = keep.tile([P, Z], U32, align_bytes=64)
+        nc.sync.dma_start(xr_w[:].bitcast(I32), xr_words[0].rearrange("p n t -> p (n t)").bitcast(I32))
+        l4 = load_list(offs4, "l4")
+        l5 = load_list(offs5, "l5")
+        l6 = load_list(offs6, "l6")
         wb_w = keep.tile([P, N], U32, align_bytes=64)
         nc.sync.dma_start(wb_w[:].bitcast(I32), wb_words[0].rearrange("p n t -> p (n t)").bitcast(I32))
-        load_scales(wb_scales, wb_s)
+        load_scales(xr_scales, xr_s, "xr_stage")
+        load_scales(ws_scales, ws_s, "ws_stage")
+        load_scales(wb_scales, wb_s, "wb_stage")
+        sa_t = load_factor(nc.gpsimd, sa, "sa_t")
+        sb_t = load_factor(nc.gpsimd, sb, "sb_t")
 
         xcd = [keep.tile([P, U], F32, name="xcd%d" % t) for t in range(PACK)]
         wc = keep.tile([P, PACK, R], BF16, align_bytes=64)
@@ -102,17 +105,15 @@ def tile_picked_respelled_codes_one_boardmixed_reminder_plain_kernel(
         def gather_wc(t):
             nc.scalar.activation(wc[:, t, :], ua_p[t][:].indirect(l3[:]), ACT.Copy, scale=ha_t[:, t : t + 1])
 
-        gather_xcd(0)
-        gather_xc(0, 0)
-        gather_wc(0)
-        gather_xcd(1)
-        gather_xc(0, 1)
-        for t in (1, 2, 3):
-            gather_wc(t)
-        for t in (2, 3):
+        for t in (0, 1):
             gather_xcd(t)
+            gather_wc(t)
+        for gather in (gather_wc, gather_xcd):
+            for t in (2, 3):
+                gather(t)
+        for t in range(PACK):
             gather_xc(0, t)
-        xc.append(keep.tile([P, PACK, HALF], BF16, name="xc1", tag="ta3", align_bytes=64))
+        xc.append(keep.tile([P, PACK, HALF], BF16, name="xc1", align_bytes=64))
         for t in range(PACK):
             gather_xc(1, t)
 
@@ -133,7 +134,7 @@ def tile_picked_respelled_codes_one_boardmixed_reminder_plain_kernel(
             xc_w = keep.tile([P, HALF], U32, name="xc_w%d" % h, align_bytes=64)
             xc_s = keep.tile([P, HALF], U8, name="xc_s%d" % h, align_bytes=64)
             nc.vector.quantize_mx(xc_w[:].bitcast(FP8X4), xc_s[:], xc_i[:].rearrange("p c j -> p (c j)"))
-            for pair in range(2):
+            for pair in (1, 0):
                 bank = psum.tile([P, 2, HALF], F32, name="a_ps%d%d" % (h, pair))
                 for e in range(2):
                     cols = slice((2 * pair + e) * P, (2 * pair + e + 1) * P)
@@ -142,7 +143,7 @@ def tile_picked_respelled_codes_one_boardmixed_reminder_plain_kernel(
                         rhs=xc_w[:].bitcast(FP8X4), rhs_scale=xc_s[:], start=True, stop=True,
                     )
                 a_sb[h, pair] = keep.tile([P, 2, HALF], F32, name="a_sb%d%d" % (h, pair))
-                if pair == 0:
+                if h == 0:
                     nc.vector.tensor_copy(a_sb[h, pair][:], bank[:])
                 else:
                     nc.scalar.copy(a_sb[h, pair][:], bank[:])
@@ -169,9 +170,9 @@ def tile_picked_respelled_codes_one_boardmixed_reminder_plain_kernel(
         scatter(0, 3, True)
         scatter(0, 0, False)
         scatter(0, 2, True)
-        scatter(1, 0, False)
-        scatter(1, 3, True)
         scatter(0, 1, False)
+        scatter(1, 3, True)
+        scatter(1, 0, False)
         scatter(1, 1, False)
         scatter(1, 2, False)
 
@@ -186,7 +187,7 @@ def tile_picked_respelled_codes_one_boardmixed_reminder_plain_kernel(
                 rhs=xg_w[:].bitcast(FP8X4), rhs_scale=xg_s[:], start=True, stop=False,
             )
 
-        for t in (0, 3, 1, 2):
+        for t in (3, 0, 1, 2):
             read_board(t)
 
         hid = keep.tile([P, O, PACK], BF16, align_bytes=64)

@@ -52,6 +52,8 @@ def tile_picked_respelled_codes_one_boardmixed_reminder_plain_kernel(
             for q in range(4):
                 nc.vector.tensor_copy(tile[32 * q : 32 * q + 4, :].bitcast(I32), stage[:, q, :])
 
+        warm = keep.tile([P, 2], F32)
+        nc.vector.memset(warm[:, 0:1], 0.0)
         xr_s = keep.tile([P, Z], U8, align_bytes=64)
         ws_s = keep.tile([P, N], U8, align_bytes=64)
         wb_s = keep.tile([P, N], U8, align_bytes=64)
@@ -90,6 +92,8 @@ def tile_picked_respelled_codes_one_boardmixed_reminder_plain_kernel(
         load_scales(wb_scales, wb_s, "wb_stage")
         sa_t = load_factor(nc.gpsimd, sa, "sa_t")
         sb_t = load_factor(nc.gpsimd, sb, "sb_t")
+
+        nc.scalar.activation(warm[:, 1:2], warm[:, 0:1], ACT.Copy)
 
         xcd = [keep.tile([P, U], F32, name="xcd%d" % t) for t in range(PACK)]
         wc = keep.tile([P, PACK, R], BF16, align_bytes=64)

@@ -45,12 +45,9 @@ def tile_picked_respelled_codes_one_boardmixed_reminder_plain_kernel(
             nc.sync.dma_start(tile[:], src.rearrange("(p t) c -> t p c", t=PACK)[t])
             return tile
 
-        def load_scales(src, tile, name):
-            words = src.shape[2] // 4
-            stage = keep.tile([4, 4, words], I32, name=name)
-            nc.gpsimd.dma_start(stage[:], src[0].bitcast(I32).rearrange("(q r) n -> r q n", r=4))
+        def load_scales(src, tile):
             for q in range(4):
-                nc.vector.tensor_copy(tile[32 * q : 32 * q + 4, :].bitcast(I32), stage[:, q, :])
+                nc.sync.dma_start(tile[32 * q : 32 * q + 4, :].bitcast(I32), src[0, 4 * q : 4 * q + 4, :].bitcast(I32))
 
         warm = keep.tile([P, 2], F32)
         nc.vector.memset(warm[:, 0:1], 0.0)
@@ -72,26 +69,26 @@ def tile_picked_respelled_codes_one_boardmixed_reminder_plain_kernel(
         l3 = load_list(offs3, "l3")
         ua_p[0] = load_plane(ua, 0, "ua0")
         ta_p[1] = load_plane(ta, 1, "ta1")
-        l7 = load_list(offs7, "l7")
         for t in (1, 2, 3):
             ua_p[t] = load_plane(ua, t, "ua%d" % t)
-        ws_w = keep.tile([P, 2 * N], U8, align_bytes=64)
-        nc.sync.dma_start(ws_w[:].bitcast(I32), ws_words[0].bitcast(I32))
         for t in (2, 3):
             ta_p[t] = load_plane(ta, t, "ta%d" % t)
         l2 = load_list(offs2, "l2")
+        l7 = load_list(offs7, "l7")
         xr_w = keep.tile([P, Z], U32, align_bytes=64)
         nc.sync.dma_start(xr_w[:].bitcast(I32), xr_words[0].rearrange("p n t -> p (n t)").bitcast(I32))
         l4 = load_list(offs4, "l4")
-        l5 = load_list(offs5, "l5")
-        l6 = load_list(offs6, "l6")
-        wb_w = keep.tile([P, N], U32, align_bytes=64)
-        nc.sync.dma_start(wb_w[:].bitcast(I32), wb_words[0].rearrange("p n t -> p (n t)").bitcast(I32))
-        load_scales(xr_scales, xr_s, "xr_stage")
-        load_scales(ws_scales, ws_s, "ws_stage")
-        load_scales(wb_scales, wb_s, "wb_stage")
         sa_t = load_factor(nc.gpsimd, sa, "sa_t")
         sb_t = load_factor(nc.gpsimd, sb, "sb_t")
+        l5 = load_list(offs5, "l5")
+        l6 = load_list(offs6, "l6")
+        load_scales(xr_scales, xr_s)
+        ws_w = keep.tile([P, 2 * N], U8, align_bytes=64)
+        nc.sync.dma_start(ws_w[:].bitcast(I32), ws_words[0].bitcast(I32))
+        wb_w = keep.tile([P, N], U32, align_bytes=64)
+        nc.sync.dma_start(wb_w[:].bitcast(I32), wb_words[0].rearrange("p n t -> p (n t)").bitcast(I32))
+        load_scales(ws_scales, ws_s)
+        load_scales(wb_scales, wb_s)
 
         nc.scalar.activation(warm[:, 1:2], warm[:, 0:1], ACT.Copy)
 
@@ -146,7 +143,7 @@ def tile_picked_respelled_codes_one_boardmixed_reminder_plain_kernel(
                         bank[:, e, :], lhsT=wc_w[:, cols].bitcast(FP8X4), lhsT_scale=wc_s[:, cols],
                         rhs=xc_w[:].bitcast(FP8X4), rhs_scale=xc_s[:], start=True, stop=True,
                     )
-                a_sb[h, pair] = keep.tile([P, 2, HALF], F32, name="a_sb%d%d" % (h, pair))
+                a_sb[h, pair] = keep.tile([P, 2, HALF], F32, name="a_sb%d%d" % (h, pair), align_bytes=64)
                 if h == 0:
                     nc.vector.tensor_copy(a_sb[h, pair][:], bank[:])
                 else:
@@ -160,10 +157,9 @@ def tile_picked_respelled_codes_one_boardmixed_reminder_plain_kernel(
             else:
                 nc.vector.tensor_copy(board[t][:].indirect(l4[:, cols]), src)
 
-        diff = keep.tile([P, PACK, O], F32)
 
         def read_board(t):
-            one = keep.tile([P, O], F32, name="one%d" % t)
+            one = keep.tile([P, O], F32, name="one%d" % t, align_bytes=64)
             eight = keep.tile([P, O], F32, name="eight%d" % t)
             nc.scalar.activation(one[:], board[t][:].indirect(l5[:]), ACT.Copy, scale=sa_t[:, t : t + 1])
             nc.scalar.activation(eight[:], board[t][:].indirect(l6[:]), ACT.Copy, scale=sb_t[:, t : t + 1])
@@ -176,12 +172,13 @@ def tile_picked_respelled_codes_one_boardmixed_reminder_plain_kernel(
         scatter(0, 2, True)
         scatter(0, 1, False)
         scatter(1, 3, True)
+        scatter(1, 2, False)
         scatter(1, 0, False)
         scatter(1, 1, False)
-        scatter(1, 2, False)
 
+        diff = keep.tile([P, PACK, O], F32, tag="xr_s", align_bytes=64)
         xg_w = keep.tile([P, O], U32, align_bytes=64)
-        xg_s = keep.tile([P, O], U8, align_bytes=64)
+        xg_s = keep.tile([P, O], U8, tag="a_sb10", align_bytes=64)
         nc.vector.tensor_copy(xg_w[:], xr_w[:].indirect(l7[:]))
         nc.vector.tensor_copy(xg_s[:], xr_s[:].indirect(l7[:]))
         y_ps = [psum.tile([P, O], F32, name="y_ps%d" % h) for h in range(2)]
@@ -191,7 +188,7 @@ def tile_picked_respelled_codes_one_boardmixed_reminder_plain_kernel(
                 rhs=xg_w[:].bitcast(FP8X4), rhs_scale=xg_s[:], start=True, stop=False,
             )
 
-        for t in (3, 0, 1, 2):
+        for t in (3, 2, 0, 1):
             read_board(t)
 
         hid = keep.tile([P, O, PACK], BF16, align_bytes=64)

from contextlib import ExitStack

import concourse.mybir as mybir

K, J, R, T, U, F, C, O, N, S, Z = 512, 256, 512, 1024, 512, 1024, 512, 128, 256, 512, 1024
FLOPS = 2 * K * R * J + 2 * R * N * O + 2 * S * N * O

F32 = mybir.dt.float32
BF16 = mybir.dt.bfloat16
I32 = mybir.dt.int32
U32 = mybir.dt.uint32
U16 = mybir.dt.uint16
U8 = mybir.dt.uint8
FP8X4 = mybir.dt.float8_e4m3fn_x4
FP4X4 = mybir.dt.float4_e2m1fn_x4
ACT = mybir.ActivationFunctionType
ALU = mybir.AluOpType

P = 128
PACK = 4
HALF = J // 2


def tile_picked_respelled_codes_one_boardmixed_reminder_plain_kernel(
    tc, ta, ga, gb, ua, ha, sa, sb, wb_words, wb_scales, xr_words, xr_scales, ws_words, ws_scales,
    offs, offs2, offs3, offs4, offs5, offs6, offs7, out,
):
    nc = tc.nc
    with ExitStack() as ctx:
        keep = ctx.enter_context(tc.tile_pool(name="keep", bufs=1))
        psum = ctx.enter_context(tc.psum_pool(name="psum", bufs=1))

        def load_list(src, name):
            tile = keep.tile(list(src.shape), U16, name=name)
            nc.sync.dma_start(tile[:], src)
            return tile

        def load_factor(queue, src, name):
            tile = keep.tile([P, PACK], F32, name=name)
            queue.dma_start(tile[:], src.rearrange("(p t) o -> p (t o)", t=PACK))
            return tile

        def load_plane(src, t, name):
            tile = keep.tile([P, src.shape[1]], F32, name=name, align_bytes=64)
            nc.sync.dma_start(tile[:], src.rearrange("(p t) c -> t p c", t=PACK)[t])
            return tile

        def load_scales(src, tile):
            for q in range(4):
                nc.sync.dma_start(tile[32 * q : 32 * q + 4, :].bitcast(I32), src[0, 4 * q : 4 * q + 4, :].bitcast(I32))

        warm = keep.tile([P, 2], F32)
        nc.vector.memset(warm[:, 0:1], 0.0)
        xr_s = keep.tile([P, Z], U8, align_bytes=64)
        ws_s = keep.tile([P, N], U8, align_bytes=64)
        wb_s = keep.tile([P, N], U8, align_bytes=64)
        for tile in (xr_s, ws_s, wb_s):
            nc.vector.memset(tile[:].bitcast(I32), 0)
        board = [keep.tile([P, C], F32, name="board%d" % t) for t in range(PACK)]
        for t in range(PACK):
            nc.vector.memset(board[t][:], 0.0)

        ga_t = load_factor(nc.scalar, ga, "ga_t")
        l1 = load_list(offs, "l1")
        ta_p, ua_p = {}, {}
        ta_p[0] = load_plane(ta, 0, "ta0")
        ha_t = load_factor(nc.scalar, ha, "ha_t")
        gb_t = load_factor(nc.scalar, gb, "gb_t")
        l3 = load_list(offs3, "l3")
        ua_p[0] = load_plane(ua, 0, "ua0")
        ta_p[1] = load_plane(ta, 1, "ta1")
        for t in (1, 2, 3):
            ua_p[t] = load_plane(ua, t, "ua%d" % t)
        for t in (2, 3):
            ta_p[t] = load_plane(ta, t, "ta%d" % t)
        l2 = load_list(offs2, "l2")
        l7 = load_list(offs7, "l7")
        xr_w = keep.tile([P, Z], U32, align_bytes=64)
        nc.sync.dma_start(xr_w[:].bitcast(I32), xr_words[0].rearrange("p n t -> p (n t)").bitcast(I32))
        l4 = load_list(offs4, "l4")
        sa_t = load_factor(nc.gpsimd, sa, "sa_t")
        sb_t = load_factor(nc.gpsimd, sb, "sb_t")
        l5 = load_list(offs5, "l5")
        l6 = load_list(offs6, "l6")
        load_scales(xr_scales, xr_s)
        ws_w = keep.tile([P, 2 * N], U8, align_bytes=64)
        nc.sync.dma_start(ws_w[:].bitcast(I32), ws_words[0].bitcast(I32))
        wb_w = keep.tile([P, N], U32, align_bytes=64)
        nc.sync.dma_start(wb_w[:].bitcast(I32), wb_words[0].rearrange("p n t -> p (n t)").bitcast(I32))
        load_scales(ws_scales, ws_s)
        load_scales(wb_scales, wb_s)

        nc.scalar.activation(warm[:, 1:2], warm[:, 0:1], ACT.Copy)

        xcd = [keep.tile([P, U], F32, name="xcd%d" % t) for t in range(PACK)]
        wc = keep.tile([P, PACK, R], BF16, align_bytes=64)
        xc = [keep.tile([P, PACK, HALF], BF16, name="xc0", align_bytes=64)]

        def gather_xcd(t):
            nc.scalar.activation(xcd[t][:], ta_p[t][:].indirect(l1[:]), ACT.Copy, scale=ga_t[:, t : t + 1])

        def gather_xc(h, t):
            cols = slice(h * HALF // 16, (h + 1) * HALF // 16)
            nc.scalar.activation(xc[h][:, t, :], xcd[t][:].indirect(l2[:, cols]), ACT.Copy, scale=gb_t[:, t : t + 1])

        def gather_wc(t):
            nc.scalar.activation(wc[:, t, :], ua_p[t][:].indirect(l3[:]), ACT.Copy, scale=ha_t[:, t : t + 1])

        for t in (0, 1):
            gather_xcd(t)
            gather_wc(t)
        for gather in (gather_wc, gather_xcd):
            for t in (2, 3):
                gather(t)
        for t in range(PACK):
            gather_xc(0, t)
        xc.append(keep.tile([P, PACK, HALF], BF16, name="xc1", align_bytes=64))
        for t in range(PACK):
            gather_xc(1, t)

        wc_i = keep.tile([P, R * PACK], BF16, align_bytes=64)
        nc.vector.tensor_copy(
            wc_i[:].rearrange("p (t m i j) -> p m t i j", t=PACK, i=2, j=PACK),
            wc[:].rearrange("p j (m i t) -> p m t i j", i=2, t=PACK),
        )
        wc_w = keep.tile([P, R], U32, align_bytes=64)
        wc_s = keep.tile([P, R], U8, align_bytes=64)
        nc.vector.quantize_mx(wc_w[:].bitcast(FP8X4), wc_s[:], wc_i[:])

        a_sb = {}

        def first_product(h):
            xc_i = keep.tile([P, HALF, PACK], BF16, name="xc_i%d" % h, align_bytes=64)
            nc.vector.tensor_copy(xc_i[:], xc[h][:].rearrange("p j c -> p c j"))
            xc_w = keep.tile([P, HALF], U32, name="xc_w%d" % h, align_bytes=64)
            xc_s = keep.tile([P, HALF], U8, name="xc_s%d" % h, align_bytes=64)
            nc.vector.quantize_mx(xc_w[:].bitcast(FP8X4), xc_s[:], xc_i[:].rearrange("p c j -> p (c j)"))
            for pair in (1, 0):
                bank = psum.tile([P, 2, HALF], F32, name="a_ps%d%d" % (h, pair))
                for e in range(2):
                    cols = slice((2 * pair + e) * P, (2 * pair + e + 1) * P)
                    nc.tensor.matmul_mx(
                        bank[:, e, :], lhsT=wc_w[:, cols].bitcast(FP8X4), lhsT_scale=wc_s[:, cols],
                        rhs=xc_w[:].bitcast(FP8X4), rhs_scale=xc_s[:], start=True, stop=True,
                    )
                a_sb[h, pair] = keep.tile([P, 2, HALF], F32, name="a_sb%d%d" % (h, pair), align_bytes=64)
                if h == 0:
                    nc.vector.tensor_copy(a_sb[h, pair][:], bank[:])
                else:
                    nc.scalar.copy(a_sb[h, pair][:], bank[:])

        def scatter(h, t, on_scalar):
            cols = slice(h * HALF // 16, (h + 1) * HALF // 16)
            src = a_sb[h, t // 2][:, t % 2, :]
            if on_scalar:
                nc.scalar.activation(board[t][:].indirect(l4[:, cols]), src, ACT.Copy)
            else:
                nc.vector.tensor_copy(board[t][:].indirect(l4[:, cols]), src)


        def read_board(t):
            one = keep.tile([P, O], F32, name="one%d" % t, align_bytes=64)
            eight = keep.tile([P, O], F32, name="eight%d" % t)
            nc.scalar.activation(one[:], board[t][:].indirect(l5[:]), ACT.Copy, scale=sa_t[:, t : t + 1])
            nc.scalar.activation(eight[:], board[t][:].indirect(l6[:]), ACT.Copy, scale=sb_t[:, t : t + 1])
            nc.vector.tensor_tensor(diff[:, t, :], one[:], eight[:], ALU.subtract)

        first_product(0)
        first_product(1)
        scatter(0, 3, True)
        scatter(0, 0, False)
        scatter(0, 2, True)
        scatter(0, 1, False)
        scatter(1, 3, True)
        scatter(1, 2, False)
        scatter(1, 0, False)
        scatter(1, 1, False)

        diff = keep.tile([P, PACK, O], F32, tag="xr_s", align_bytes=64)
        xg_w = keep.tile([P, O], U32, align_bytes=64)
        xg_s = keep.tile([P, O], U8, tag="a_sb10", align_bytes=64)
        nc.vector.tensor_copy(xg_w[:], xr_w[:].indirect(l7[:]))
        nc.vector.tensor_copy(xg_s[:], xr_s[:].indirect(l7[:]))
        y_ps = [psum.tile([P, O], F32, name="y_ps%d" % h) for h in range(2)]
        for h in range(2):
            nc.tensor.matmul_mx(
                y_ps[h][:], lhsT=ws_w[:, 2 * h * P : 2 * (h + 1) * P].bitcast(FP4X4), lhsT_scale=ws_s[:, h * P : (h + 1) * P],
                rhs=xg_w[:].bitcast(FP8X4), rhs_scale=xg_s[:], start=True, stop=False,
            )

        for t in (3, 2, 0, 1):
            read_board(t)

        hid = keep.tile([P, O, PACK], BF16, align_bytes=64)
        by_place = diff[:].rearrange("p t o -> p o t")
        nc.scalar.activation(hid[:, : O // 2, :], by_place[:, : O // 2, :], ACT.Abs)
        nc.vector.scalar_tensor_tensor(
            hid[:, O // 2 :, :], by_place[:, O // 2 :, :], -1.0, by_place[:, O // 2 :, :], ALU.mult, ALU.max
        )
        hid_w = keep.tile([P, O], U32, align_bytes=64)
        hid_s = keep.tile([P, O], U8, align_bytes=64)
        nc.vector.quantize_mx(hid_w[:].bitcast(FP8X4), hid_s[:], hid[:].rearrange("p o t -> p (o t)"))
        for h in range(2):
            cols = slice(h * P, (h + 1) * P)
            nc.tensor.matmul_mx(
                y_ps[h][:], lhsT=wb_w[:, cols].bitcast(FP8X4), lhsT_scale=wb_s[:, cols],
                rhs=hid_w[:].bitcast(FP8X4), rhs_scale=hid_s[:], start=False, stop=True,
            )
            y_sb = keep.tile([P, O], F32, name="y_sb%d" % h)
            if h == 0:
                nc.vector.tensor_copy(y_sb[:], y_ps[h][:])
                nc.sync.dma_start(out[cols, :], y_sb[:])
            else:
                nc.scalar.copy(y_sb[:], y_ps[h][:])
                nc.scalar.dma_start(out[cols, :], y_sb[:])
